import numpy as np, ml_dtypes
CORES = [1,7,41,47,81,87,121,127]
N = 8
KB, QP = 2, 256
def setup_inputs(rng):
    return {"q": rng.standard_normal((N, 128, QP), dtype=np.float32).astype(ml_dtypes.bfloat16), "k": rng.standard_normal((N, 128, KB * 128), dtype=np.float32).astype(ml_dtypes.bfloat16), "v": rng.standard_normal((N, 128, KB * 128), dtype=np.float32).astype(ml_dtypes.bfloat16)}
def reference(q, k, v):
    Q, K, V = q.astype(np.float64), k.astype(np.float64), v.astype(np.float64)
    y = np.zeros((N, 128, QP))
    for r in range(N):
        for j in range(r + 1):
            for b in range(KB):
                S = np.maximum(K[j][:, 128 * b:128 * b + 128].T @ Q[r], 0.0)
                y[r] += V[j][:, 128 * b:128 * b + 128].T @ S
    return {"y": y.astype(ml_dtypes.bfloat16 if q.dtype != np.float64 else np.float64)}

@@ -1,0 +1,214 @@
+from concourse.bass import DstId, RemoteDMATransfer
+from concourse.mybir import AluOpType
+
+NBLK = 12
+LOOK = 2
+CHIP_INDEX = {0: 0, 5: 1, 10: 2, 15: 3}
+
+SCRATCH = {
+    "kv": ("sbuf", [128, 8 * 512], "bfloat16"),
+    "qs": ("sbuf", [128, 8 * 256], "bfloat16"),
+    "osb": ("sbuf", [128, 8 * 256], "bfloat16"),
+    "pin": ("sbuf", [128, 3 * 256], "bfloat16"),
+    "sb": ("sbuf", [128, NBLK * 256], "bfloat16"),
+    "zero": ("sbuf", [128, 256], "float32"),
+    "yout": ("sbuf", [128, 256], "bfloat16"),
+    "ps0": ("psum", [128, 512], "float32"),
+    "ps1": ("psum", [128, 512], "float32"),
+    "ps2": ("psum", [128, 512], "float32"),
+    "ps3": ("psum", [128, 512], "float32"),
+    "pay": ("psum", [128, 512], "float32"),
+    "pao": ("psum", [128, 512], "float32"),
+}
+SEMAPHORES = (["ldq", "ldk", "ldv", "sent", "zs", "ody", "odo", "ev", "ad0", "ad1", "ad2", "st"]
+              + ["kv%d" % j for j in range(8)] + ["q%d" % r for r in range(8)] + ["p%d" % c for c in range(3)]
+              + ["s%d" % i for i in range(NBLK)] + ["r%d" % i for i in range(NBLK)])
+
+CALLS = {
+    1:   [("kv", 0, 0, (7, 2, 6)), ("o", 4)],
+    7:   [("kv", 1, 1, (1, 2, 6)), ("kv", 1, 1, (121,)), ("o", 5)],
+    2:   [("kv", 0, 1, (41,)), ("o", 7)],
+    6:   [("kv", 0, 0, (121,)), ("o", 3)],
+    41:  [("kv", 2, 2, (47, 42)), ("o", 6)],
+    47:  [("q", 3, (6,)), ("kv", 3, 3, (41, 42)), ("kv", 3, 3, (81,)), ("o", 7)],
+    42:  [("kv", 2, 2, (81,)), ("o", 5)],
+    81:  [("q", 4, (1,)), ("kv", 4, 4, (87, 82))],
+    87:  [("q", 5, (7, 42)), ("kv", 5, 5, (121,)), ("o", 7)],
+    82:  [("kv", 4, 4, (121,))],
+    121: [("q", 6, (41,)), ("kv", 6, 6, (127,))],
+    127: [("q", 7, (2, 47, 87))],
+}
+BURSTS = {
+    1:   [[("y", 0, 0)], [("o", 4, 0), ("o", 4, 1)]],
+    7:   [[("y", 1, 1)], [("o", 5, 0), ("o", 5, 1)], [("y", 1, 0)]],
+    2:   [[("o", 7, 0), ("o", 7, 1)]],
+    6:   [[("o", 3, 0), ("o", 3, 1)]],
+    41:  [[("y", 2, 2)], [("o", 6, 2), ("o", 6, 3)], [("y", 2, 0), ("y", 2, 1)]],
+    47:  [[("y", 3, 3)], [("o", 7, 2), ("o", 7, 3)], [("y", 3, 2)]],
+    42:  [[("o", 5, 2), ("o", 5, 3)]],
+    81:  [[("y", 4, 4)], [("y", 4, 3)], [("y", 4, 2)]],
+    87:  [[("y", 5, 5)], [("o", 7, 4), ("o", 7, 5)], [("y", 5, 4)]],
+    121: [[("y", 6, 6)], [("y", 6, 5)], [("y", 6, 1)], [("y", 6, 4)], [("y", 6, 0)]],
+    127: [[("y", 7, 7)], [("y", 7, 6)]],
+}
+PARTS = {0: (), 1: (), 2: (), 3: (0,), 4: (0,), 5: (0, 1), 6: (1,), 7: (2, 1, 0)}
+LOADS = {0: ("kq", "v"), 1: ("kq", "v"), 2: ("kq", "v"), 3: ("qv", "k"), 4: ("qv", "k"), 5: ("qv", "k"),
+         6: ("qv", "k"), 7: ("qv", "k")}
+
+
+def _pop(m):
+    return bin(m).count("1")
+
+
+def _mask(src, dests):
+    return 0xFFFF if all(d // 8 == src // 8 for d in dests) else 0x00FF
+
+
+def _arrivals():
+    arr = {}
+    for src, calls in CALLS.items():
+        for c in calls:
+            if c[0] == "kv":
+                n = _pop(_mask(src, c[3]))
+                for d in c[3]:
+                    for j in range(c[1], c[2] + 1):
+                        arr[(d, "kv", j)] = ("kv%d" % c[1], n)
+            elif c[0] == "q":
+                n = _pop(_mask(src, c[2]))
+                for d in c[2]:
+                    arr[(d, "q", c[1])] = ("q%d" % c[1], n)
+    return arr
+
+
+def rank_program(g, core, T, topo):
+    if core not in CALLS and core not in BURSTS:
+        return
+    rank = T.rank_of(core)
+    arr = _arrivals()
+    sem = T.sem
+    queues = {"g": g, "t": g.tensor, "v": g.vector, "s": g.sync, "a": g.scalar}
+    waited = {}
+
+    def wait(qn, name, val):
+        if waited.get((qn, name), 0) >= val:
+            return
+        waited[(qn, name)] = val
+        queues[qn].wait_ge(sem[name], val)
+
+    def need(qn, kind, idx):
+        if rank is not None and idx == rank:
+            if kind == "q":
+                wait(qn, "ldq", 16)
+            else:
+                wait(qn, "ldk", 16)
+                wait(qn, "ldv", 16)
+        else:
+            s, n = arr[(core, kind, idx)]
+            wait(qn, s, n)
+
+    if rank is not None:
+        for qn, what in zip(("s", "a"), LOADS[rank]):
+            for w in what:
+                if w == "q":
+                    queues[qn].dma_start(T.qs[:, rank * 256:rank * 256 + 256], T.q[:]).then_inc(sem["ldq"], 16)
+                elif w == "k":
+                    queues[qn].dma_start(T.kv[:, rank * 512:rank * 512 + 256], T.k[:]).then_inc(sem["ldk"], 16)
+                else:
+                    queues[qn].dma_start(T.kv[:, rank * 512 + 256:rank * 512 + 512], T.v[:]).then_inc(sem["ldv"], 16)
+
+    bursts = BURSTS.get(core, [])
+    tot = {}
+    for bu in bursts:
+        for (acc, r, j) in bu:
+            tot[acc] = tot.get(acc, 0) + 2
+    if bursts:
+        g.vector.memset(T.zero[:], 0.0).then_inc(sem["zs"], 1)
+        wait("v", "zs", 1)
+    seen = {}
+    i = 0
+    for bu in bursts:
+        blocks = []
+        for (acc, r, j) in bu:
+            for b in (0, 1):
+                blocks.append((i, acc, r, j, b))
+                i += 1
+        n = len(blocks)
+        for t in range(n + LOOK):
+            if t < n:
+                (x, acc, r, j, b) = blocks[t]
+                need("t", "q", r)
+                need("t", "kv", j)
+                if x >= 4:
+                    wait("t", "r%d" % (x - 4), 1)
+                c0 = j * 512 + b * 128
+                g.tensor.matmul(T["ps%d" % (x % 4)][:, 0:256], T.kv[:, c0:c0 + 128],
+                                T.qs[:, r * 256:r * 256 + 256], True, True).then_inc(sem["s%d" % x], 1)
+            if t >= LOOK:
+                (x, acc, r, j, b) = blocks[t - LOOK]
+                wait("t", "r%d" % x, 1)
+                k = seen.get(acc, 0)
+                seen[acc] = k + 1
+                c0 = j * 512 + 256 + b * 128
+                g.tensor.matmul(T["pa" + acc][:, 0:256], T.kv[:, c0:c0 + 128],
+                                T.sb[:, x * 256:x * 256 + 256], k == 0, k == tot[acc] - 1).then_inc(sem["od" + acc], 1)
+        for (x, acc, r, j, b) in blocks:
+            wait("v", "s%d" % x, 1)
+            g.vector.tensor_tensor(T.sb[:, x * 256:x * 256 + 256], T["ps%d" % (x % 4)][:, 0:256], T.zero[:],
+                                   AluOpType.max).then_inc(sem["r%d" % x], 1)
+        if bu[0][0] == "o":
+            r = bu[0][1]
+            wait("v", "odo", tot["o"])
+            g.vector.tensor_copy(T.osb[:, r * 256:r * 256 + 256], T.pao[:, 0:256]).then_inc(sem["ev"], 1)
+
+    if rank is not None:
+        wait("v", "ody", tot["y"])
+        parts = PARTS[rank]
+        last = "ad0"
+        if not parts:
+            g.vector.tensor_copy(T.yout[:], T.pay[:, 0:256]).then_inc(sem["ad0"], 1)
+        for a, c in enumerate(parts):
+            wait("v", "p%d" % c, 8)
+            if a > 0:
+                wait("v", "ad%d" % (a - 1), 1)
+            src = T.pay[:, (a % 2) * 256:(a % 2) * 256 + 256]
+            dst = T.yout[:] if a == len(parts) - 1 else T.pay[:, ((a + 1) % 2) * 256:((a + 1) % 2) * 256 + 256]
+            last = "ad%d" % a
+            g.vector.tensor_tensor(dst, src, T.pin[:, c * 256:c * 256 + 256], AluOpType.add).then_inc(sem[last], 1)
+        wait("s", last, 1)
+        g.sync.dma_start(T.y[:], T.yout[:]).then_inc(sem["st"], 16)
+        wait("s", "st", 16)
+
+    total = 0
+    for c in CALLS.get(core, []):
+        if c[0] == "kv":
+            for j in range(c[1], c[2] + 1):
+                need("g", "kv", j)
+            src = T.kv[:, c[1] * 512:(c[2] + 1) * 512]
+            dst = src
+            rs = "kv%d" % c[1]
+            dests = c[3]
+        elif c[0] == "q":
+            need("g", "q", c[1])
+            src = T.qs[:, c[1] * 256:c[1] * 256 + 256]
+            dst = src
+            rs = "q%d" % c[1]
+            dests = c[2]
+        else:
+            wait("g", "ev", 1)
+            ci = CHIP_INDEX[core // 8]
+            src = T.osb[:, c[1] * 256:c[1] * 256 + 256]
+            dst = T.pin[:, ci * 256:ci * 256 + 256]
+            rs = "p%d" % ci
+            dests = (T.cores[c[1]],)
+        m = _mask(core, dests)
+        if len(dests) == 1:
+            rid, pid, _se = topo.addr(dests[0])
+            g.remote_dma(out_ap=dst, in_ap=src, remote_sem=sem[rs], local_sem=sem["sent"], pid=pid, routing_id=rid,
+                         dma_engine_mask=m)
+        else:
+            ids = [DstId(rid=topo.addr(d)[0], pnc=topo.addr(d)[1]) for d in dests]
+            g.remote_dma_fused([RemoteDMATransfer(dst_ids=ids, dma_engine_mask=m, remote_sem=sem[rs], srcs=[src],
+                                                  dsts=[dst for _d in dests], alu_op=0)], local_sem=sem["sent"])
+        total += _pop(m)
+    if total:
+        wait("g", "sent", total)

@@ -25,16 +25,17 @@ SEMAPHORES = (["ldq", "ldk", "ldv", "sent", "zs", "ody", "odo", "ev", "ad0", "ad
               + ["s%d" % i for i in range(NBLK)] + ["r%d" % i for i in range(NBLK)])
 
 CALLS = {
-    1:   [("kv", 0, 0, (7, 2, 6)), ("o", 4)],
-    7:   [("kv", 1, 1, (1, 2, 6)), ("kv", 1, 1, (121,)), ("o", 5)],
-    2:   [("kv", 0, 1, (41,)), ("o", 7)],
-    6:   [("kv", 0, 0, (121,)), ("o", 3)],
-    41:  [("kv", 2, 2, (47, 42)), ("o", 6)],
+    1:   [("kv", 0, 0, (2, 6, 7, 3)), ("o", 4)],
+    7:   [("kv", 1, 1, (6, 2, 1)), ("kv", 1, 1, (121,)), ("o", 5)],
+    2:   [("kv", 0, 0, (121,)), ("o", 7)],
+    3:   [("kv", 0, 0, (41,))],
+    6:   [("kv", 1, 1, (41,)), ("o", 3)],
+    41:  [("kv", 2, 2, (42, 47)), ("o", 6)],
     47:  [("q", 3, (6,)), ("kv", 3, 3, (41, 42)), ("kv", 3, 3, (81,)), ("o", 7)],
     42:  [("kv", 2, 2, (81,)), ("o", 5)],
-    81:  [("q", 4, (1,)), ("kv", 4, 4, (87, 82))],
+    81:  [("kv", 4, 4, (114, 87)), ("q", 4, (1,))],
     87:  [("q", 5, (7, 42)), ("kv", 5, 5, (121,)), ("o", 7)],
-    82:  [("kv", 4, 4, (121,))],
+    114: [("kv", 4, 4, (121,))],
     121: [("q", 6, (41,)), ("kv", 6, 6, (127,))],
     127: [("q", 7, (2, 47, 87))],
 }
@@ -43,16 +44,16 @@ BURSTS = {
     7:   [[("y", 1, 1)], [("o", 5, 0), ("o", 5, 1)], [("y", 1, 0)]],
     2:   [[("o", 7, 0), ("o", 7, 1)]],
     6:   [[("o", 3, 0), ("o", 3, 1)]],
-    41:  [[("y", 2, 2)], [("o", 6, 2), ("o", 6, 3)], [("y", 2, 0), ("y", 2, 1)]],
+    41:  [[("y", 2, 2)], [("o", 6, 2), ("o", 6, 3)], [("y", 2, 1)], [("y", 2, 0)]],
     47:  [[("y", 3, 3)], [("o", 7, 2), ("o", 7, 3)], [("y", 3, 2)]],
     42:  [[("o", 5, 2), ("o", 5, 3)]],
     81:  [[("y", 4, 4)], [("y", 4, 3)], [("y", 4, 2)]],
     87:  [[("y", 5, 5)], [("o", 7, 4), ("o", 7, 5)], [("y", 5, 4)]],
-    121: [[("y", 6, 6)], [("y", 6, 5)], [("y", 6, 1)], [("y", 6, 4)], [("y", 6, 0)]],
+    121: [[("y", 6, 6)], [("y", 6, 5), ("y", 6, 0), ("y", 6, 1), ("y", 6, 4)]],
     127: [[("y", 7, 7)], [("y", 7, 6)]],
 }
-PARTS = {0: (), 1: (), 2: (), 3: (0,), 4: (0,), 5: (0, 1), 6: (1,), 7: (2, 1, 0)}
-LOADS = {0: ("kq", "v"), 1: ("kq", "v"), 2: ("kq", "v"), 3: ("qv", "k"), 4: ("qv", "k"), 5: ("qv", "k"),
+PARTS = {0: (), 1: (), 2: (), 3: (0,), 4: (0,), 5: (0, 1), 6: (1,), 7: (1, 0, 2)}
+LOADS = {0: ("kq", "v"), 1: ("kq", "v"), 2: ("kq", "v"), 3: ("qv", "k"), 4: ("kq", "v"), 5: ("qv", "k"),
          6: ("qv", "k"), 7: ("qv", "k")}
 
 
@@ -60,8 +61,12 @@ def _pop(m):
     return bin(m).count("1")
 
 
-def _mask(src, dests):
-    return 0xFFFF if all(d // 8 == src // 8 for d in dests) else 0x00FF
+def _parts(src, dests):
+    on = tuple(d for d in dests if d // 8 == src // 8)
+    off = tuple(d for d in dests if d // 8 != src // 8)
+    if on and off:
+        return [(off, 0x00FF), (on, 0xFF00)]
+    return [(dests, 0xFFFF if on else 0x00FF)]
 
 
 def _arrivals():
@@ -69,14 +74,14 @@ def _arrivals():
     for src, calls in CALLS.items():
         for c in calls:
             if c[0] == "kv":
-                n = _pop(_mask(src, c[3]))
-                for d in c[3]:
-                    for j in range(c[1], c[2] + 1):
-                        arr[(d, "kv", j)] = ("kv%d" % c[1], n)
+                for ds, m in _parts(src, c[3]):
+                    for d in ds:
+                        for j in range(c[1], c[2] + 1):
+                            arr[(d, "kv", j)] = ("kv%d" % c[1], _pop(m))
             elif c[0] == "q":
-                n = _pop(_mask(src, c[2]))
-                for d in c[2]:
-                    arr[(d, "q", c[1])] = ("q%d" % c[1], n)
+                for ds, m in _parts(src, c[2]):
+                    for d in ds:
+                        arr[(d, "q", c[1])] = ("q%d" % c[1], _pop(m))
     return arr
 
 
@@ -200,15 +205,16 @@ def rank_program(g, core, T, topo):
             dst = T.pin[:, ci * 256:ci * 256 + 256]
             rs = "p%d" % ci
             dests = (T.cores[c[1]],)
-        m = _mask(core, dests)
+        trs = _parts(core, dests)
         if len(dests) == 1:
             rid, pid, _se = topo.addr(dests[0])
             g.remote_dma(out_ap=dst, in_ap=src, remote_sem=sem[rs], local_sem=sem["sent"], pid=pid, routing_id=rid,
-                         dma_engine_mask=m)
+                         dma_engine_mask=trs[0][1])
         else:
-            ids = [DstId(rid=topo.addr(d)[0], pnc=topo.addr(d)[1]) for d in dests]
-            g.remote_dma_fused([RemoteDMATransfer(dst_ids=ids, dma_engine_mask=m, remote_sem=sem[rs], srcs=[src],
-                                                  dsts=[dst for _d in dests], alu_op=0)], local_sem=sem["sent"])
-        total += _pop(m)
+            g.remote_dma_fused([RemoteDMATransfer(dst_ids=[DstId(rid=topo.addr(d)[0], pnc=topo.addr(d)[1]) for d in ds],
+                                                  dma_engine_mask=m, remote_sem=sem[rs], srcs=[src],
+                                                  dsts=[dst for _d in ds], alu_op=0) for ds, m in trs],
+                               local_sem=sem["sent"])
+        total += sum(_pop(m) for _ds, m in trs)
     if total:
         wait("g", "sent", total)

@@ -20,7 +20,7 @@ SCRATCH = {
     "pay": ("psum", [128, 512], "float32"),
     "pao": ("psum", [128, 512], "float32"),
 }
-SEMAPHORES = (["ldq", "ldk", "ldv", "sent", "zs", "ody", "odo", "ev", "ad0", "ad1", "ad2", "st"]
+SEMAPHORES = (["ldq", "ldk", "ldv", "gldq", "gldk", "gldv", "sent", "zs", "ody", "odo", "ev", "ad0", "ad1", "ad2", "st"]
               + ["kv%d" % j for j in range(8)] + ["q%d" % r for r in range(8)] + ["p%d" % c for c in range(3)]
               + ["s%d" % i for i in range(NBLK)] + ["r%d" % i for i in range(NBLK)])
 
@@ -53,8 +53,8 @@ BURSTS = {
     127: [[("y", 7, 7)], [("y", 7, 6)]],
 }
 PARTS = {0: (), 1: (), 2: (), 3: (0,), 4: (0,), 5: (0, 1), 6: (1,), 7: (1, 0, 2)}
-LOADS = {0: ("kq", "v"), 1: ("kq", "v"), 2: ("kq", "v"), 3: ("qv", "k"), 4: ("kq", "v"), 5: ("qv", "k"),
-         6: ("qv", "k"), 7: ("qv", "k")}
+LOADS = {0: ("kq", "v", ""), 1: ("kq", "v", ""), 2: ("kq", "v", ""), 3: ("q", "k", "v"), 4: ("k", "v", "q"),
+         5: ("q", "k", "v"), 6: ("qkv", "", ""), 7: ("qkv", "", "")}
 
 
 def _pop(m):
@@ -93,6 +93,7 @@ def rank_program(g, core, T, topo):
     sem = T.sem
     queues = {"g": g, "t": g.tensor, "v": g.vector, "s": g.sync, "a": g.scalar}
     waited = {}
+    ldsem = {}
 
     def wait(qn, name, val):
         if waited.get((qn, name), 0) >= val:
@@ -103,23 +104,24 @@ def rank_program(g, core, T, topo):
     def need(qn, kind, idx):
         if rank is not None and idx == rank:
             if kind == "q":
-                wait(qn, "ldq", 16)
+                wait(qn, ldsem["q"], 16)
             else:
-                wait(qn, "ldk", 16)
-                wait(qn, "ldv", 16)
+                wait(qn, ldsem["k"], 16)
+                wait(qn, ldsem["v"], 16)
         else:
             s, n = arr[(core, kind, idx)]
             wait(qn, s, n)
 
     if rank is not None:
-        for qn, what in zip(("s", "a"), LOADS[rank]):
+        for qn, what in zip(("s", "a", "g"), LOADS[rank]):
             for w in what:
+                ldsem[w] = ("gld" if qn == "g" else "ld") + w
                 if w == "q":
-                    queues[qn].dma_start(T.qs[:, rank * 256:rank * 256 + 256], T.q[:]).then_inc(sem["ldq"], 16)
+                    queues[qn].dma_start(T.qs[:, rank * 256:rank * 256 + 256], T.q[:]).then_inc(sem[ldsem[w]], 16)
                 elif w == "k":
-                    queues[qn].dma_start(T.kv[:, rank * 512:rank * 512 + 256], T.k[:]).then_inc(sem["ldk"], 16)
+                    queues[qn].dma_start(T.kv[:, rank * 512:rank * 512 + 256], T.k[:]).then_inc(sem[ldsem[w]], 16)
                 else:
-                    queues[qn].dma_start(T.kv[:, rank * 512 + 256:rank * 512 + 512], T.v[:]).then_inc(sem["ldv"], 16)
+                    queues[qn].dma_start(T.kv[:, rank * 512 + 256:rank * 512 + 512], T.v[:]).then_inc(sem[ldsem[w]], 16)
 
     bursts = BURSTS.get(core, [])
     tot = {}

from concourse.bass import DstId, RemoteDMATransfer
from concourse.mybir import AluOpType

NBLK = 12
LOOK = 2
CHIP_INDEX = {0: 0, 5: 1, 10: 2, 15: 3}

SCRATCH = {
    "kv": ("sbuf", [128, 8 * 512], "bfloat16"),
    "qs": ("sbuf", [128, 8 * 256], "bfloat16"),
    "osb": ("sbuf", [128, 8 * 256], "bfloat16"),
    "pin": ("sbuf", [128, 3 * 256], "bfloat16"),
    "sb": ("sbuf", [128, NBLK * 256], "bfloat16"),
    "zero": ("sbuf", [128, 256], "float32"),
    "yout": ("sbuf", [128, 256], "bfloat16"),
    "ps0": ("psum", [128, 512], "float32"),
    "ps1": ("psum", [128, 512], "float32"),
    "ps2": ("psum", [128, 512], "float32"),
    "ps3": ("psum", [128, 512], "float32"),
    "pay": ("psum", [128, 512], "float32"),
    "pao": ("psum", [128, 512], "float32"),
}
SEMAPHORES = (["ldq", "ldk", "ldv", "gldq", "gldk", "gldv", "sent", "zs", "ody", "odo", "ev", "ad0", "ad1", "ad2", "st"]
              + ["kv%d" % j for j in range(8)] + ["q%d" % r for r in range(8)] + ["p%d" % c for c in range(3)]
              + ["s%d" % i for i in range(NBLK)] + ["r%d" % i for i in range(NBLK)])

CALLS = {
    1:   [("kv", 0, 0, (2, 6, 7, 3)), ("o", 4)],
    7:   [("kv", 1, 1, (6, 2, 1)), ("kv", 1, 1, (121,)), ("o", 5)],
    2:   [("kv", 0, 0, (121,)), ("o", 7)],
    3:   [("kv", 0, 0, (41,))],
    6:   [("kv", 1, 1, (41,)), ("o", 3)],
    41:  [("kv", 2, 2, (42, 47)), ("o", 6)],
    47:  [("q", 3, (6,)), ("kv", 3, 3, (41, 42)), ("kv", 3, 3, (81,)), ("o", 7)],
    42:  [("kv", 2, 2, (81,)), ("o", 5)],
    81:  [("kv", 4, 4, (114, 87)), ("q", 4, (1,))],
    87:  [("q", 5, (7, 42)), ("kv", 5, 5, (121,)), ("o", 7)],
    114: [("kv", 4, 4, (121,))],
    121: [("q", 6, (41,)), ("kv", 6, 6, (127,))],
    127: [("q", 7, (2, 47, 87))],
}
BURSTS = {
    1:   [[("y", 0, 0)], [("o", 4, 0), ("o", 4, 1)]],
    7:   [[("y", 1, 1)], [("o", 5, 0), ("o", 5, 1)], [("y", 1, 0)]],
    2:   [[("o", 7, 0), ("o", 7, 1)]],
    6:   [[("o", 3, 0), ("o", 3, 1)]],
    41:  [[("y", 2, 2)], [("o", 6, 2), ("o", 6, 3)], [("y", 2, 1)], [("y", 2, 0)]],
    47:  [[("y", 3, 3)], [("o", 7, 2), ("o", 7, 3)], [("y", 3, 2)]],
    42:  [[("o", 5, 2), ("o", 5, 3)]],
    81:  [[("y", 4, 4)], [("y", 4, 3)], [("y", 4, 2)]],
    87:  [[("y", 5, 5)], [("o", 7, 4), ("o", 7, 5)], [("y", 5, 4)]],
    121: [[("y", 6, 6)], [("y", 6, 5), ("y", 6, 0), ("y", 6, 1), ("y", 6, 4)]],
    127: [[("y", 7, 7)], [("y", 7, 6)]],
}
PARTS = {0: (), 1: (), 2: (), 3: (0,), 4: (0,), 5: (0, 1), 6: (1,), 7: (1, 0, 2)}
LOADS = {0: ("kq", "v", ""), 1: ("kq", "v", ""), 2: ("kq", "v", ""), 3: ("q", "k", "v"), 4: ("k", "v", "q"),
         5: ("q", "k", "v"), 6: ("qkv", "", ""), 7: ("qkv", "", "")}


def _pop(m):
    return bin(m).count("1")


def _parts(src, dests):
    on = tuple(d for d in dests if d // 8 == src // 8)
    off = tuple(d for d in dests if d // 8 != src // 8)
    if on and off:
        return [(off, 0x00FF), (on, 0xFF00)]
    return [(dests, 0xFFFF if on else 0x00FF)]


def _arrivals():
    arr = {}
    for src, calls in CALLS.items():
        for c in calls:
            if c[0] == "kv":
                for ds, m in _parts(src, c[3]):
                    for d in ds:
                        for j in range(c[1], c[2] + 1):
                            arr[(d, "kv", j)] = ("kv%d" % c[1], _pop(m))
            elif c[0] == "q":
                for ds, m in _parts(src, c[2]):
                    for d in ds:
                        arr[(d, "q", c[1])] = ("q%d" % c[1], _pop(m))
    return arr


def rank_program(g, core, T, topo):
    if core not in CALLS and core not in BURSTS:
        return
    rank = T.rank_of(core)
    arr = _arrivals()
    sem = T.sem
    queues = {"g": g, "t": g.tensor, "v": g.vector, "s": g.sync, "a": g.scalar}
    waited = {}
    ldsem = {}

    def wait(qn, name, val):
        if waited.get((qn, name), 0) >= val:
            return
        waited[(qn, name)] = val
        queues[qn].wait_ge(sem[name], val)

    def need(qn, kind, idx):
        if rank is not None and idx == rank:
            if kind == "q":
                wait(qn, ldsem["q"], 16)
            else:
                wait(qn, ldsem["k"], 16)
                wait(qn, ldsem["v"], 16)
        else:
            s, n = arr[(core, kind, idx)]
            wait(qn, s, n)

    if rank is not None:
        for qn, what in zip(("s", "a", "g"), LOADS[rank]):
            for w in what:
                ldsem[w] = ("gld" if qn == "g" else "ld") + w
                if w == "q":
                    queues[qn].dma_start(T.qs[:, rank * 256:rank * 256 + 256], T.q[:]).then_inc(sem[ldsem[w]], 16)
                elif w == "k":
                    queues[qn].dma_start(T.kv[:, rank * 512:rank * 512 + 256], T.k[:]).then_inc(sem[ldsem[w]], 16)
                else:
                    queues[qn].dma_start(T.kv[:, rank * 512 + 256:rank * 512 + 512], T.v[:]).then_inc(sem[ldsem[w]], 16)

    bursts = BURSTS.get(core, [])
    tot = {}
    for bu in bursts:
        for (acc, r, j) in bu:
            tot[acc] = tot.get(acc, 0) + 2
    if bursts:
        g.vector.memset(T.zero[:], 0.0).then_inc(sem["zs"], 1)
        wait("v", "zs", 1)
    seen = {}
    i = 0
    for bu in bursts:
        blocks = []
        for (acc, r, j) in bu:
            for b in (0, 1):
                blocks.append((i, acc, r, j, b))
                i += 1
        n = len(blocks)
        for t in range(n + LOOK):
            if t < n:
                (x, acc, r, j, b) = blocks[t]
                need("t", "q", r)
                need("t", "kv", j)
                if x >= 4:
                    wait("t", "r%d" % (x - 4), 1)
                c0 = j * 512 + b * 128
                g.tensor.matmul(T["ps%d" % (x % 4)][:, 0:256], T.kv[:, c0:c0 + 128],
                                T.qs[:, r * 256:r * 256 + 256], True, True).then_inc(sem["s%d" % x], 1)
            if t >= LOOK:
                (x, acc, r, j, b) = blocks[t - LOOK]
                wait("t", "r%d" % x, 1)
                k = seen.get(acc, 0)
                seen[acc] = k + 1
                c0 = j * 512 + 256 + b * 128
                g.tensor.matmul(T["pa" + acc][:, 0:256], T.kv[:, c0:c0 + 128],
                                T.sb[:, x * 256:x * 256 + 256], k == 0, k == tot[acc] - 1).then_inc(sem["od" + acc], 1)
        for (x, acc, r, j, b) in blocks:
            wait("v", "s%d" % x, 1)
            g.vector.tensor_tensor(T.sb[:, x * 256:x * 256 + 256], T["ps%d" % (x % 4)][:, 0:256], T.zero[:],
                                   AluOpType.max).then_inc(sem["r%d" % x], 1)
        if bu[0][0] == "o":
            r = bu[0][1]
            wait("v", "odo", tot["o"])
            g.vector.tensor_copy(T.osb[:, r * 256:r * 256 + 256], T.pao[:, 0:256]).then_inc(sem["ev"], 1)

    if rank is not None:
        wait("v", "ody", tot["y"])
        parts = PARTS[rank]
        last = "ad0"
        if not parts:
            g.vector.tensor_copy(T.yout[:], T.pay[:, 0:256]).then_inc(sem["ad0"], 1)
        for a, c in enumerate(parts):
            wait("v", "p%d" % c, 8)
            if a > 0:
                wait("v", "ad%d" % (a - 1), 1)
            src = T.pay[:, (a % 2) * 256:(a % 2) * 256 + 256]
            dst = T.yout[:] if a == len(parts) - 1 else T.pay[:, ((a + 1) % 2) * 256:((a + 1) % 2) * 256 + 256]
            last = "ad%d" % a
            g.vector.tensor_tensor(dst, src, T.pin[:, c * 256:c * 256 + 256], AluOpType.add).then_inc(sem[last], 1)
        wait("s", last, 1)
        g.sync.dma_start(T.y[:], T.yout[:]).then_inc(sem["st"], 16)
        wait("s", "st", 16)

    total = 0
    for c in CALLS.get(core, []):
        if c[0] == "kv":
            for j in range(c[1], c[2] + 1):
                need("g", "kv", j)
            src = T.kv[:, c[1] * 512:(c[2] + 1) * 512]
            dst = src
            rs = "kv%d" % c[1]
            dests = c[3]
        elif c[0] == "q":
            need("g", "q", c[1])
            src = T.qs[:, c[1] * 256:c[1] * 256 + 256]
            dst = src
            rs = "q%d" % c[1]
            dests = c[2]
        else:
            wait("g", "ev", 1)
            ci = CHIP_INDEX[core // 8]
            src = T.osb[:, c[1] * 256:c[1] * 256 + 256]
            dst = T.pin[:, ci * 256:ci * 256 + 256]
            rs = "p%d" % ci
            dests = (T.cores[c[1]],)
        trs = _parts(core, dests)
        if len(dests) == 1:
            rid, pid, _se = topo.addr(dests[0])
            g.remote_dma(out_ap=dst, in_ap=src, remote_sem=sem[rs], local_sem=sem["sent"], pid=pid, routing_id=rid,
                         dma_engine_mask=trs[0][1])
        else:
            g.remote_dma_fused([RemoteDMATransfer(dst_ids=[DstId(rid=topo.addr(d)[0], pnc=topo.addr(d)[1]) for d in ds],
                                                  dma_engine_mask=m, remote_sem=sem[rs], srcs=[src],
                                                  dsts=[dst for _d in ds], alu_op=0) for ds, m in trs],
                               local_sem=sem["sent"])
        total += sum(_pop(m) for _ds, m in trs)
    if total:
        wait("g", "sent", total)
